import numpy as np
import ml_dtypes


def mxq(x, axis, fmt="e4m3"):
    dtype, down = {"e4m3": (ml_dtypes.float8_e4m3fn, 7), "e5m2": (ml_dtypes.float8_e5m2, 14)}[fmt]
    v = np.moveaxis(np.asarray(x, np.float32).astype(ml_dtypes.bfloat16).astype(np.float64), axis, -1)
    blocks = v.reshape(v.shape[:-1] + (-1, 32))
    amax = np.abs(blocks).max(-1, keepdims=True)
    byte = np.maximum(np.where(amax > 0, np.frexp(amax)[1] - 1 + 127, 0) - down, 1)
    scale = np.exp2(byte - 127.0)
    codes = (blocks / scale).astype(np.float32).astype(dtype).astype(np.float64)
    return np.moveaxis((codes * scale).reshape(v.shape), -1, axis)


WIDE = False


def mx_kscale(k):
    if not WIDE:
        return np.ones(k)
    levels = np.array([10, -10, 5, -5, 0])
    if k % 512:
        return np.exp2(np.random.permutation(np.resize(levels, k // 32))).repeat(32)
    a = np.empty((k // 512, 16))
    for p in range(k // 512):
        a[p, :8] = np.random.permutation(np.resize(levels, 8))
        for g in range(8):
            far = levels[np.abs(levels - a[p, g]) >= 10]
            a[p, g + 8] = far[np.random.randint(len(far))]
    return np.exp2(a.ravel()).repeat(32)


def f64(x):
    return np.asarray(x).astype(np.float64)


def striped(idx):
    return np.tile(np.asarray(idx).reshape(-1, 16).T, (8, 1)).astype(np.uint16)


def unstriped(offs):
    return offs[:16].T.reshape(-1).astype(np.int64)


G, K, T, D, M = 128, 32, 2048, 512, 256


def setup_inputs():
    n = np.random.standard_normal
    s = mx_kscale(D)[:, None]
    grid = lambda x: np.round(x * 32) / 32
    x = grid(n((D, T))) * s
    idx = np.random.randint(0, T, (G, K))
    return {
        "xT": x.astype(np.float32),
        "w": (n((D, M)) / np.sqrt(D * K) / s).astype(np.float32),
        "offs": striped(idx.reshape(-1)),
    }


def reference(xT, w, offs):
    x = f64(xT)[:, unstriped(offs)]
    y = mxq(f64(w), 0, "e4m3").T @ mxq(x.reshape(D, G, K).sum(-1), 0, "e4m3")
    return y

@@ -1,0 +1,151 @@
+from contextlib import ExitStack
+
+import concourse.mybir as mybir
+
+F32 = mybir.dt.float32
+BF16 = mybir.dt.bfloat16
+U32 = mybir.dt.uint32
+U16 = mybir.dt.uint16
+U8 = mybir.dt.uint8
+FP8X4 = mybir.dt.float8_e4m3fn_x4
+COPY = mybir.ActivationFunctionType.Copy
+ADD = mybir.AluOpType.add
+AXIS_X = mybir.AxisListType.X
+
+P = 128
+BAGS, K, T, D, M = 128, 32, 2048, 512, 256
+FLOPS = 2 * BAGS * D * M
+
+NG = 64
+NS = 28
+CHUNKS = (512, 512, 512, 512)
+PIECES = (("G", 0, 16), ("S", 64, 28), ("G", 16, 24), ("G", 40, 24), ("V", 92, 36))
+
+
+def tile_attend_bag_kernel(tc, xT, w, offs, out):
+    nc = tc.nc
+    with ExitStack() as ctx:
+        held = ctx.enter_context(tc.tile_pool(name="held", bufs=1))
+        spin = ctx.enter_context(tc.tile_pool(name="spin", bufs=8))
+        psum = ctx.enter_context(tc.psum_pool(name="psum", bufs=1))
+
+        offsets = held.tile([P, BAGS * K // 16], U16, name="offsets")
+        nc.sync.dma_start(offsets[:], offs)
+
+        x_rows = xT.rearrange("(p t) n -> p t n", t=4)
+        table = []
+        raw = []
+        for q in range(2):
+            chunks = []
+            n0 = 0
+            for c, width in enumerate(CHUNKS):
+                r = held.tile([P, 2, width], F32, name=f"raw{q}_{c}")
+                nc.sync.dma_start(r[:], x_rows[:, 2 * q : 2 * q + 2, n0 : n0 + width])
+                chunks.append((n0, width, r))
+                n0 += width
+            raw.append(chunks)
+            pair = held.tile([P, T, 2], BF16, name=f"pair{q}", align_bytes=64)
+            table.append(pair)
+        w_raw = held.tile([P, 4, M], F32, name="w_raw")
+        nc.sync.dma_start(w_raw[:], w.rearrange("(p t) m -> p t m", t=4))
+
+        w_mix = held.tile([P, M, 4], BF16, name="w_mix", align_bytes=64)
+        w_codes = held.tile([P, M], U32, name="w_codes", align_bytes=64)
+        w_scales = held.tile([P, M], U8, name="w_scales", align_bytes=64)
+        e_mix = held.tile([P, BAGS, 4], BF16, name="e_mix", align_bytes=64)
+        e_codes = held.tile([P, BAGS], U32, name="e_codes", align_bytes=64)
+        e_scales = held.tile([P, BAGS], U8, name="e_scales", align_bytes=64)
+        s_sums = held.tile([P, NS, 4], F32, name="s_sums")
+
+        def cast(q, n0, width, r, halves):
+            h = width // 2
+            if halves:
+                nc.vector.tensor_copy(table[q][:, n0 : n0 + h, :], r[:, :, 0:h].rearrange("p t n -> p n t"))
+                nc.scalar.copy(table[q][:, n0 + h : n0 + width, :], r[:, :, h:width].rearrange("p t n -> p n t"))
+            else:
+                nc.scalar.copy(table[q][:, n0 : n0 + width, :], r[:].rearrange("p t n -> p n t"))
+
+        got = {}
+
+        def gather(q, i):
+            owner, b0, nb = PIECES[i]
+            g = held.tile([P, nb * K, 2], BF16, name=f"got{q}_{i}", align_bytes=64)
+            got[q, i] = g
+            window = table[q][:].rearrange("p n t -> p (n t)").bitcast(U32)
+            dst = g[:].rearrange("p n t -> p (n t)").bitcast(U32)
+            nc.vector.tensor_copy(dst, window.indirect(offsets[:, 2 * b0 : 2 * (b0 + nb)]))
+
+        def tree(q, i):
+            owner, b0, nb = PIECES[i]
+            src = got[q, i][:].rearrange("p (b j) t -> p b j t", j=K)
+            n = K // 2
+            while n >= 1:
+                if n > 1:
+                    dst_t = held.tile([P, nb, n, 2], F32, name=f"tree{q}_{i}_{n}")
+                    dst = dst_t[:]
+                    nc.gpsimd.tensor_tensor(dst, src[:, :, 0:n, :], src[:, :, n : 2 * n, :], ADD)
+                    src = dst
+                else:
+                    nc.gpsimd.tensor_tensor(
+                        e_mix[:, b0 : b0 + nb, 2 * q : 2 * q + 2], src[:, :, 0, :], src[:, :, 1, :], ADD
+                    )
+                n //= 2
+
+        def accumulate(q, i):
+            owner, b0, nb = PIECES[i]
+            src = got[q, i][:].rearrange("p (b j) t -> p b j t", j=K)
+            for b in range(nb):
+                for t in range(2):
+                    junk = spin.tile([P, K], BF16, name="junk")
+                    col = s_sums[:, b0 - NG + b, 2 * q + t : 2 * q + t + 1]
+                    nc.scalar.activation(junk[:], src[:, b, :, t], COPY, accum_out=col)
+
+        def reduce(q, i):
+            owner, b0, nb = PIECES[i]
+            src = got[q, i][:].rearrange("p (b j) t -> p b t j", j=K)
+            nc.vector.tensor_reduce(e_mix[:, b0 : b0 + nb, 2 * q : 2 * q + 2], src, AXIS_X, ADD)
+
+        with nc.allow_low_precision("each bag's float32 sum is rounded once to bfloat16"):
+            for n0, width, r in raw[0]:
+                cast(0, n0, width, r, True)
+            for q in range(2):
+                for i in range(len(PIECES)):
+                    if q == 1 and PIECES[i][0] == "V":
+                        nc.vector.quantize_mx(
+                            out=w_codes[:].bitcast(FP8X4),
+                            scales=w_scales[:],
+                            in_=w_mix[:].rearrange("p m t -> p (m t)"),
+                        )
+                    gather(q, i)
+                    if PIECES[i][0] == "G":
+                        tree(q, i)
+                    if PIECES[i][0] == "S":
+                        if q == 0:
+                            for n0, width, r in raw[1]:
+                                cast(1, n0, width, r, False)
+                            nc.scalar.copy(w_mix[:], w_raw[:].rearrange("p t m -> p m t"))
+                        accumulate(q, i)
+            last = len(PIECES) - 1
+            reduce(0, last)
+            reduce(1, last)
+            nc.scalar.copy(e_mix[:, NG : NG + NS, :], s_sums[:])
+            nc.vector.quantize_mx(
+                out=e_codes[:].bitcast(FP8X4), scales=e_scales[:], in_=e_mix[:].rearrange("p b t -> p (b t)")
+            )
+            result = held.tile([P, 2, BAGS], F32, name="result")
+            for h in range(2):
+                acc = psum.tile([P, BAGS], F32, name=f"acc{h}")
+                nc.tensor.matmul_mx(
+                    out=acc[:],
+                    lhsT=w_codes[:, h * P : (h + 1) * P].bitcast(FP8X4),
+                    lhsT_scale=w_scales[:, h * P : (h + 1) * P],
+                    rhs=e_codes[:].bitcast(FP8X4),
+                    rhs_scale=e_scales[:],
+                    start=True,
+                    stop=True,
+                )
+                if h == 0:
+                    nc.vector.tensor_copy(result[:, h, :], acc[:])
+                else:
+                    nc.scalar.copy(result[:, h, :], acc[:])
+            nc.sync.dma_start(out.rearrange("(h m) g -> m h g", h=2), result[:])

@@ -16,17 +16,20 @@ P = 128
 BAGS, K, T, D, M = 128, 32, 2048, 512, 256
 FLOPS = 2 * BAGS * D * M
 
-NG = 64
+NG = 44
 NS = 28
-CHUNKS = (512, 512, 512, 512)
-PIECES = (("G", 0, 16), ("S", 64, 28), ("G", 16, 24), ("G", 40, 24), ("V", 92, 36))
+CHUNKS = (640, 640, 512, 256)
+PIECES = (("G", 0, 16), ("G", 16, 28), ("S", 44, 28), ("V", 72, 28), ("V", 100, 28))
+ORDERS = (
+    (("gather", 0), ("gather", 1), ("gather", 2), ("gather", 3), ("gather", 4), ("reduce", 3), ("reduce", 4)),
+    (("gather", 0), ("gather", 2), ("gather", 1), ("gather", 3), ("gather", 4), ("reduce", 3), ("reduce", 4)),
+)
 
 
 def tile_attend_bag_kernel(tc, xT, w, offs, out):
     nc = tc.nc
     with ExitStack() as ctx:
         held = ctx.enter_context(tc.tile_pool(name="held", bufs=1))
-        spin = ctx.enter_context(tc.tile_pool(name="spin", bufs=8))
         psum = ctx.enter_context(tc.psum_pool(name="psum", bufs=1))
 
         offsets = held.tile([P, BAGS * K // 16], U16, name="offsets")
@@ -58,7 +61,7 @@ def tile_attend_bag_kernel(tc, xT, w, offs, out):
         s_sums = held.tile([P, NS, 4], F32, name="s_sums")
 
         def cast(q, n0, width, r, halves):
-            h = width // 2
+            h = 5 * width // 8
             if halves:
                 nc.vector.tensor_copy(table[q][:, n0 : n0 + h, :], r[:, :, 0:h].rearrange("p t n -> p n t"))
                 nc.scalar.copy(table[q][:, n0 + h : n0 + width, :], r[:, :, h:width].rearrange("p t n -> p n t"))
@@ -91,14 +94,15 @@ def tile_attend_bag_kernel(tc, xT, w, offs, out):
                     )
                 n //= 2
 
+        junk = held.tile([P, NS, 4, K], BF16, name="junk")
+
         def accumulate(q, i):
             owner, b0, nb = PIECES[i]
             src = got[q, i][:].rearrange("p (b j) t -> p b j t", j=K)
             for b in range(nb):
                 for t in range(2):
-                    junk = spin.tile([P, K], BF16, name="junk")
                     col = s_sums[:, b0 - NG + b, 2 * q + t : 2 * q + t + 1]
-                    nc.scalar.activation(junk[:], src[:, b, :, t], COPY, accum_out=col)
+                    nc.scalar.activation(junk[:, b0 - NG + b, 2 * q + t, :], src[:, b, :, t], COPY, accum_out=col)
 
         def reduce(q, i):
             owner, b0, nb = PIECES[i]
@@ -108,26 +112,26 @@ def tile_attend_bag_kernel(tc, xT, w, offs, out):
         with nc.allow_low_precision("each bag's float32 sum is rounded once to bfloat16"):
             for n0, width, r in raw[0]:
                 cast(0, n0, width, r, True)
-            for q in range(2):
-                for i in range(len(PIECES)):
-                    if q == 1 and PIECES[i][0] == "V":
-                        nc.vector.quantize_mx(
-                            out=w_codes[:].bitcast(FP8X4),
-                            scales=w_scales[:],
-                            in_=w_mix[:].rearrange("p m t -> p (m t)"),
-                        )
-                    gather(q, i)
-                    if PIECES[i][0] == "G":
-                        tree(q, i)
-                    if PIECES[i][0] == "S":
-                        if q == 0:
-                            for n0, width, r in raw[1]:
-                                cast(1, n0, width, r, False)
-                            nc.scalar.copy(w_mix[:], w_raw[:].rearrange("p t m -> p m t"))
-                        accumulate(q, i)
-            last = len(PIECES) - 1
-            reduce(0, last)
-            reduce(1, last)
+            for q, order in enumerate(ORDERS):
+                for step, i in order:
+                    if step == "gather":
+                        gather(q, i)
+                        if PIECES[i][0] == "G":
+                            tree(q, i)
+                        if PIECES[i][0] == "S":
+                            if q == 0:
+                                for n0, width, r in raw[1]:
+                                    cast(1, n0, width, r, False)
+                                nc.scalar.copy(w_mix[:], w_raw[:].rearrange("p t m -> p m t"))
+                            accumulate(q, i)
+                    else:
+                        reduce(q, i)
+                if q == 0:
+                    nc.vector.quantize_mx(
+                        out=w_codes[:].bitcast(FP8X4),
+                        scales=w_scales[:],
+                        in_=w_mix[:].rearrange("p m t -> p (m t)"),
+                    )
             nc.scalar.copy(e_mix[:, NG : NG + NS, :], s_sums[:])
             nc.vector.quantize_mx(
                 out=e_codes[:].bitcast(FP8X4), scales=e_scales[:], in_=e_mix[:].rearrange("p b t -> p (b t)")

@@ -16,13 +16,30 @@ P = 128
 BAGS, K, T, D, M = 128, 32, 2048, 512, 256
 FLOPS = 2 * BAGS * D * M
 
-NG = 44
-NS = 28
-CHUNKS = (640, 640, 512, 256)
-PIECES = (("G", 0, 16), ("G", 16, 28), ("S", 44, 28), ("V", 72, 28), ("V", 100, 28))
-ORDERS = (
-    (("gather", 0), ("gather", 1), ("gather", 2), ("gather", 3), ("gather", 4), ("reduce", 3), ("reduce", 4)),
-    (("gather", 0), ("gather", 2), ("gather", 1), ("gather", 3), ("gather", 4), ("reduce", 3), ("reduce", 4)),
+NG = 56
+NS = 32
+CHUNKS = ((640, 640, 512, 256), (768, 768, 512))
+PLAN = (
+    ("gather", 0, 0, 24),
+    ("G1", 0, 0, 24),
+    ("gather", 0, 24, 32),
+    ("G1", 0, 24, 32),
+    ("G", 0, 0, NG),
+    ("cast", 0, 0, 0),
+    ("gather", 0, 56, 32),
+    ("S", 0, 56, 32),
+    ("gather", 0, 88, 40),
+    ("gather", 1, 0, 24),
+    ("G1", 1, 0, 24),
+    ("gather", 1, 56, 32),
+    ("S", 1, 56, 32),
+    ("gather", 1, 24, 32),
+    ("G1", 1, 24, 32),
+    ("G", 1, 0, NG),
+    ("V", 0, 88, 40),
+    ("w", 0, 0, 0),
+    ("gather", 1, 88, 40),
+    ("V", 1, 88, 40),
 )
 
 
@@ -41,7 +58,7 @@ def tile_attend_bag_kernel(tc, xT, w, offs, out):
         for q in range(2):
             chunks = []
             n0 = 0
-            for c, width in enumerate(CHUNKS):
+            for c, width in enumerate(CHUNKS[q]):
                 r = held.tile([P, 2, width], F32, name=f"raw{q}_{c}")
                 nc.sync.dma_start(r[:], x_rows[:, 2 * q : 2 * q + 2, n0 : n0 + width])
                 chunks.append((n0, width, r))
@@ -68,70 +85,67 @@ def tile_attend_bag_kernel(tc, xT, w, offs, out):
             else:
                 nc.scalar.copy(table[q][:, n0 : n0 + width, :], r[:].rearrange("p t n -> p n t"))
 
-        got = {}
-
-        def gather(q, i):
-            owner, b0, nb = PIECES[i]
-            g = held.tile([P, nb * K, 2], BF16, name=f"got{q}_{i}", align_bytes=64)
-            got[q, i] = g
-            window = table[q][:].rearrange("p n t -> p (n t)").bitcast(U32)
-            dst = g[:].rearrange("p n t -> p (n t)").bitcast(U32)
-            nc.vector.tensor_copy(dst, window.indirect(offsets[:, 2 * b0 : 2 * (b0 + nb)]))
-
-        def tree(q, i):
-            owner, b0, nb = PIECES[i]
-            src = got[q, i][:].rearrange("p (b j) t -> p b j t", j=K)
-            n = K // 2
-            while n >= 1:
-                if n > 1:
-                    dst_t = held.tile([P, nb, n, 2], F32, name=f"tree{q}_{i}_{n}")
-                    dst = dst_t[:]
-                    nc.gpsimd.tensor_tensor(dst, src[:, :, 0:n, :], src[:, :, n : 2 * n, :], ADD)
-                    src = dst
-                else:
-                    nc.gpsimd.tensor_tensor(
-                        e_mix[:, b0 : b0 + nb, 2 * q : 2 * q + 2], src[:, :, 0, :], src[:, :, 1, :], ADD
-                    )
-                n //= 2
-
+        got = [held.tile([P, BAGS * K, 2], BF16, name=f"got{q}", align_bytes=64) for q in range(2)]
         junk = held.tile([P, NS, 4, K], BF16, name="junk")
 
-        def accumulate(q, i):
-            owner, b0, nb = PIECES[i]
-            src = got[q, i][:].rearrange("p (b j) t -> p b j t", j=K)
+        def gather(q, b0, nb):
+            window = table[q][:].rearrange("p n t -> p (n t)").bitcast(U32)
+            dst = got[q][:, b0 * K : (b0 + nb) * K, :].rearrange("p n t -> p (n t)").bitcast(U32)
+            nc.vector.tensor_copy(dst, window.indirect(offsets[:, 2 * b0 : 2 * (b0 + nb)]))
+
+        def bags(q, b0, nb):
+            return got[q][:, b0 * K : (b0 + nb) * K, :].rearrange("p (b j) t -> p b j t", j=K)
+
+        halves = [held.tile([P, NG, K // 2, 2], F32, name=f"half{q}") for q in range(2)]
+
+        def first_level(q, b0, nb):
+            src = bags(q, b0, nb)
+            nc.gpsimd.tensor_tensor(
+                halves[q][:, b0 : b0 + nb, :, :], src[:, :, 0 : K // 2, :], src[:, :, K // 2 : K, :], ADD
+            )
+
+        def tree(q, b0, nb):
+            src = halves[q][:]
+            n = K // 4
+            while n > 1:
+                dst = held.tile([P, nb, n, 2], F32, name=f"tree{q}_{n}")
+                nc.gpsimd.tensor_tensor(dst[:], src[:, :, 0:n, :], src[:, :, n : 2 * n, :], ADD)
+                src = dst[:]
+                n //= 2
+            nc.gpsimd.tensor_tensor(
+                e_mix[:, b0 : b0 + nb, 2 * q : 2 * q + 2], src[:, :, 0, :], src[:, :, 1, :], ADD
+            )
+
+        def accumulate(q, b0, nb):
+            src = bags(q, b0, nb)
             for b in range(nb):
                 for t in range(2):
-                    col = s_sums[:, b0 - NG + b, 2 * q + t : 2 * q + t + 1]
-                    nc.scalar.activation(junk[:, b0 - NG + b, 2 * q + t, :], src[:, b, :, t], COPY, accum_out=col)
+                    s = b0 - NG + b
+                    col = s_sums[:, s, 2 * q + t : 2 * q + t + 1]
+                    nc.scalar.activation(junk[:, s, 2 * q + t, :], src[:, b, :, t], COPY, accum_out=col)
 
-        def reduce(q, i):
-            owner, b0, nb = PIECES[i]
-            src = got[q, i][:].rearrange("p (b j) t -> p b t j", j=K)
+        def reduce(q, b0, nb):
+            src = bags(q, b0, nb).rearrange("p b j t -> p b t j")
             nc.vector.tensor_reduce(e_mix[:, b0 : b0 + nb, 2 * q : 2 * q + 2], src, AXIS_X, ADD)
 
+        def prepare(q, b0, nb):
+            for n0, width, r in raw[1]:
+                cast(1, n0, width, r, False)
+            nc.scalar.copy(w_mix[:], w_raw[:].rearrange("p t m -> p m t"))
+
+        def quantise_w(q, b0, nb):
+            nc.vector.quantize_mx(
+                out=w_codes[:].bitcast(FP8X4),
+                scales=w_scales[:],
+                in_=w_mix[:].rearrange("p m t -> p (m t)"),
+            )
+
+        step = {"gather": gather, "G1": first_level, "G": tree, "S": accumulate, "V": reduce, "cast": prepare, "w": quantise_w}
         with nc.allow_low_precision("each bag's float32 sum is rounded once to bfloat16"):
             for n0, width, r in raw[0]:
                 cast(0, n0, width, r, True)
-            for q, order in enumerate(ORDERS):
-                for step, i in order:
-                    if step == "gather":
-                        gather(q, i)
-                        if PIECES[i][0] == "G":
-                            tree(q, i)
-                        if PIECES[i][0] == "S":
-                            if q == 0:
-                                for n0, width, r in raw[1]:
-                                    cast(1, n0, width, r, False)
-                                nc.scalar.copy(w_mix[:], w_raw[:].rearrange("p t m -> p m t"))
-                            accumulate(q, i)
-                    else:
-                        reduce(q, i)
-                if q == 0:
-                    nc.vector.quantize_mx(
-                        out=w_codes[:].bitcast(FP8X4),
-                        scales=w_scales[:],
-                        in_=w_mix[:].rearrange("p m t -> p (m t)"),
-                    )
+            for name, q, b0, nb in PLAN:
+                step[name](q, b0, nb)
             nc.scalar.copy(e_mix[:, NG : NG + NS, :], s_sums[:])
             nc.vector.quantize_mx(
                 out=e_codes[:].bitcast(FP8X4), scales=e_scales[:], in_=e_mix[:].rearrange("p b t -> p (b t)")

from contextlib import ExitStack

import concourse.mybir as mybir

F32 = mybir.dt.float32
BF16 = mybir.dt.bfloat16
U32 = mybir.dt.uint32
U16 = mybir.dt.uint16
U8 = mybir.dt.uint8
FP8X4 = mybir.dt.float8_e4m3fn_x4
COPY = mybir.ActivationFunctionType.Copy
ADD = mybir.AluOpType.add
AXIS_X = mybir.AxisListType.X

P = 128
BAGS, K, T, D, M = 128, 32, 2048, 512, 256
FLOPS = 2 * BAGS * D * M

NG = 56
NS = 32
CHUNKS = ((640, 640, 512, 256), (768, 768, 512))
PLAN = (
    ("gather", 0, 0, 24),
    ("G1", 0, 0, 24),
    ("gather", 0, 24, 32),
    ("G1", 0, 24, 32),
    ("G", 0, 0, NG),
    ("cast", 0, 0, 0),
    ("gather", 0, 56, 32),
    ("S", 0, 56, 32),
    ("gather", 0, 88, 40),
    ("gather", 1, 0, 24),
    ("G1", 1, 0, 24),
    ("gather", 1, 56, 32),
    ("S", 1, 56, 32),
    ("gather", 1, 24, 32),
    ("G1", 1, 24, 32),
    ("G", 1, 0, NG),
    ("V", 0, 88, 40),
    ("w", 0, 0, 0),
    ("gather", 1, 88, 40),
    ("V", 1, 88, 40),
)


def tile_attend_bag_kernel(tc, xT, w, offs, out):
    nc = tc.nc
    with ExitStack() as ctx:
        held = ctx.enter_context(tc.tile_pool(name="held", bufs=1))
        psum = ctx.enter_context(tc.psum_pool(name="psum", bufs=1))

        offsets = held.tile([P, BAGS * K // 16], U16, name="offsets")
        nc.sync.dma_start(offsets[:], offs)

        x_rows = xT.rearrange("(p t) n -> p t n", t=4)
        table = []
        raw = []
        for q in range(2):
            chunks = []
            n0 = 0
            for c, width in enumerate(CHUNKS[q]):
                r = held.tile([P, 2, width], F32, name=f"raw{q}_{c}")
                nc.sync.dma_start(r[:], x_rows[:, 2 * q : 2 * q + 2, n0 : n0 + width])
                chunks.append((n0, width, r))
                n0 += width
            raw.append(chunks)
            pair = held.tile([P, T, 2], BF16, name=f"pair{q}", align_bytes=64)
            table.append(pair)
        w_raw = held.tile([P, 4, M], F32, name="w_raw")
        nc.sync.dma_start(w_raw[:], w.rearrange("(p t) m -> p t m", t=4))

        w_mix = held.tile([P, M, 4], BF16, name="w_mix", align_bytes=64)
        w_codes = held.tile([P, M], U32, name="w_codes", align_bytes=64)
        w_scales = held.tile([P, M], U8, name="w_scales", align_bytes=64)
        e_mix = held.tile([P, BAGS, 4], BF16, name="e_mix", align_bytes=64)
        e_codes = held.tile([P, BAGS], U32, name="e_codes", align_bytes=64)
        e_scales = held.tile([P, BAGS], U8, name="e_scales", align_bytes=64)
        s_sums = held.tile([P, NS, 4], F32, name="s_sums")

        def cast(q, n0, width, r, halves):
            h = 5 * width // 8
            if halves:
                nc.vector.tensor_copy(table[q][:, n0 : n0 + h, :], r[:, :, 0:h].rearrange("p t n -> p n t"))
                nc.scalar.copy(table[q][:, n0 + h : n0 + width, :], r[:, :, h:width].rearrange("p t n -> p n t"))
            else:
                nc.scalar.copy(table[q][:, n0 : n0 + width, :], r[:].rearrange("p t n -> p n t"))

        got = [held.tile([P, BAGS * K, 2], BF16, name=f"got{q}", align_bytes=64) for q in range(2)]
        junk = held.tile([P, NS, 4, K], BF16, name="junk")

        def gather(q, b0, nb):
            window = table[q][:].rearrange("p n t -> p (n t)").bitcast(U32)
            dst = got[q][:, b0 * K : (b0 + nb) * K, :].rearrange("p n t -> p (n t)").bitcast(U32)
            nc.vector.tensor_copy(dst, window.indirect(offsets[:, 2 * b0 : 2 * (b0 + nb)]))

        def bags(q, b0, nb):
            return got[q][:, b0 * K : (b0 + nb) * K, :].rearrange("p (b j) t -> p b j t", j=K)

        halves = [held.tile([P, NG, K // 2, 2], F32, name=f"half{q}") for q in range(2)]

        def first_level(q, b0, nb):
            src = bags(q, b0, nb)
            nc.gpsimd.tensor_tensor(
                halves[q][:, b0 : b0 + nb, :, :], src[:, :, 0 : K // 2, :], src[:, :, K // 2 : K, :], ADD
            )

        def tree(q, b0, nb):
            src = halves[q][:]
            n = K // 4
            while n > 1:
                dst = held.tile([P, nb, n, 2], F32, name=f"tree{q}_{n}")
                nc.gpsimd.tensor_tensor(dst[:], src[:, :, 0:n, :], src[:, :, n : 2 * n, :], ADD)
                src = dst[:]
                n //= 2
            nc.gpsimd.tensor_tensor(
                e_mix[:, b0 : b0 + nb, 2 * q : 2 * q + 2], src[:, :, 0, :], src[:, :, 1, :], ADD
            )

        def accumulate(q, b0, nb):
            src = bags(q, b0, nb)
            for b in range(nb):
                for t in range(2):
                    s = b0 - NG + b
                    col = s_sums[:, s, 2 * q + t : 2 * q + t + 1]
                    nc.scalar.activation(junk[:, s, 2 * q + t, :], src[:, b, :, t], COPY, accum_out=col)

        def reduce(q, b0, nb):
            src = bags(q, b0, nb).rearrange("p b j t -> p b t j")
            nc.vector.tensor_reduce(e_mix[:, b0 : b0 + nb, 2 * q : 2 * q + 2], src, AXIS_X, ADD)

        def prepare(q, b0, nb):
            for n0, width, r in raw[1]:
                cast(1, n0, width, r, False)
            nc.scalar.copy(w_mix[:], w_raw[:].rearrange("p t m -> p m t"))

        def quantise_w(q, b0, nb):
            nc.vector.quantize_mx(
                out=w_codes[:].bitcast(FP8X4),
                scales=w_scales[:],
                in_=w_mix[:].rearrange("p m t -> p (m t)"),
            )

        step = {"gather": gather, "G1": first_level, "G": tree, "S": accumulate, "V": reduce, "cast": prepare, "w": quantise_w}
        with nc.allow_low_precision("each bag's float32 sum is rounded once to bfloat16"):
            for n0, width, r in raw[0]:
                cast(0, n0, width, r, True)
            for name, q, b0, nb in PLAN:
                step[name](q, b0, nb)
            nc.scalar.copy(e_mix[:, NG : NG + NS, :], s_sums[:])
            nc.vector.quantize_mx(
                out=e_codes[:].bitcast(FP8X4), scales=e_scales[:], in_=e_mix[:].rearrange("p b t -> p (b t)")
            )
            result = held.tile([P, 2, BAGS], F32, name="result")
            for h in range(2):
                acc = psum.tile([P, BAGS], F32, name=f"acc{h}")
                nc.tensor.matmul_mx(
                    out=acc[:],
                    lhsT=w_codes[:, h * P : (h + 1) * P].bitcast(FP8X4),
                    lhsT_scale=w_scales[:, h * P : (h + 1) * P],
                    rhs=e_codes[:].bitcast(FP8X4),
                    rhs_scale=e_scales[:],
                    start=True,
                    stop=True,
                )
                if h == 0:
                    nc.vector.tensor_copy(result[:, h, :], acc[:])
                else:
                    nc.scalar.copy(result[:, h, :], acc[:])
            nc.sync.dma_start(out.rearrange("(h m) g -> m h g", h=2), result[:])
